import numpy as np
import ml_dtypes


def mxq(x, axis, fmt="e4m3"):
    dtype, down = {"e4m3": (ml_dtypes.float8_e4m3fn, 7), "e5m2": (ml_dtypes.float8_e5m2, 14)}[fmt]
    v = np.moveaxis(np.asarray(x, np.float32).astype(ml_dtypes.bfloat16).astype(np.float64), axis, -1)
    blocks = v.reshape(v.shape[:-1] + (-1, 32))
    amax = np.abs(blocks).max(-1, keepdims=True)
    byte = np.maximum(np.where(amax > 0, np.frexp(amax)[1] - 1 + 127, 0) - down, 1)
    scale = np.exp2(byte - 127.0)
    codes = (blocks / scale).astype(np.float32).astype(dtype).astype(np.float64)
    return np.moveaxis((codes * scale).reshape(v.shape), -1, axis)


WIDE = False


def mx_kscale(k):
    if not WIDE:
        return np.ones(k)
    levels = np.array([10, -10, 5, -5, 0])
    if k % 512:
        return np.exp2(np.random.permutation(np.resize(levels, k // 32))).repeat(32)
    a = np.empty((k // 512, 16))
    for p in range(k // 512):
        a[p, :8] = np.random.permutation(np.resize(levels, 8))
        for g in range(8):
            far = levels[np.abs(levels - a[p, g]) >= 10]
            a[p, g + 8] = far[np.random.randint(len(far))]
    return np.exp2(a.ravel()).repeat(32)


def f64(x):
    return np.asarray(x).astype(np.float64)


def striped(idx):
    return np.tile(np.asarray(idx).reshape(-1, 16).T, (8, 1)).astype(np.uint16)


def unstriped(offs):
    return offs[:16].T.reshape(-1).astype(np.int64)


E2M1 = np.array([0.0, 0.5, 1.0, 1.5, 2.0, 3.0, 4.0, 6.0, -0.0, -0.5, -1.0, -1.5, -2.0, -3.0, -4.0, -6.0])


def pack_weight(w, fmt):
    k, n = w.shape
    w = f64(np.asarray(w, np.float32).astype(ml_dtypes.bfloat16)).reshape(k // 32, 32, n)
    amax = np.abs(w).max(1)
    if fmt == "e4m3":
        byte = np.frexp(amax)[1] - 1 + 127 - 7
    else:
        mant, ex = np.frexp(amax / 6.0)
        byte = np.where(mant > 0.5, ex, ex - 1) + 127
    byte = np.clip(np.where(amax > 0, byte, 1), 1, 254)
    scaled = (w * np.exp2(127.0 - byte)[:, None, :]).reshape(k, n).astype(np.float32)
    by_word = np.ascontiguousarray(scaled.reshape(k // 512, 128, 4, n).transpose(0, 1, 3, 2))
    if fmt == "e4m3":
        words = by_word.astype(ml_dtypes.float8_e4m3fn).view(np.uint8)
    else:
        c = by_word.astype(ml_dtypes.float4_e2m1fn).view(np.uint8) & 0xF
        words = (c[..., 0::2] | (c[..., 1::2] << 4)).reshape(k // 512, 128, 2 * n)
    return np.ascontiguousarray(words), np.ascontiguousarray(byte.astype(np.uint8).reshape(k // 512, 16, n))


def unpack_weight(words, scales, fmt):
    g, _, n = scales.shape
    words = np.ascontiguousarray(words).reshape(g, 128, n, -1)
    if fmt == "e4m3":
        vals = words.view(ml_dtypes.float8_e4m3fn).astype(np.float64)
    else:
        nib = np.empty((g, 128, n, 4), np.uint8)
        nib[..., 0::2] = words & 0xF
        nib[..., 1::2] = words >> 4
        vals = E2M1[nib]
    vals = vals * np.repeat(np.exp2(scales.astype(np.float64) - 127.0), 8, axis=1)[..., None]
    return vals.transpose(0, 1, 3, 2).reshape(g * 512, n)


def bf(x):
    return np.asarray(x, np.float32).astype(ml_dtypes.bfloat16)


def planes(Y):
    r, m = Y.shape
    b = f64(bf(Y)).reshape(r // 32, 32, m)
    amax = np.abs(b).max(1)
    byte = np.clip(np.where(amax > 0, np.frexp(amax)[1] - 1 + 127 - 7, 1), 1, 254)
    codes = (b * np.exp2(127.0 - byte)[:, None, :]).reshape(r, m).astype(np.float32).astype(ml_dtypes.float8_e4m3fn).view(np.uint8)
    words = codes.reshape(r // 512, 128, 4, m).transpose(0, 1, 3, 2)
    return np.ascontiguousarray(words), np.ascontiguousarray(byte.astype(np.uint8).reshape(r // 512, 16, m))


K, T, J, N = 512, 512, 512, 512


def setup_inputs():
    n = np.random.standard_normal
    idx = np.random.randint(0, T, J)
    idx2 = np.random.randint(0, T, J)
    fk = mx_kscale(K)
    wap = pack_weight(n((K, N)) * 1 / np.sqrt(K) * fk[:, None], "e2m1")
    wbp = pack_weight(n((K, N)) * 1 / np.sqrt(K) * fk[:, None], "e4m3")
    return {
        "xt": (n((K, T)) / fk[:, None]).astype(np.float32),
        "wa_words": wap[0],
        "wa_scales": wap[1],
        "wb_words": wbp[0],
        "wb_scales": wbp[1],
        "offs": striped(idx),
        "offs2": striped(idx2),
    }


def reference(xt, wa_words, wa_scales, wb_words, wb_scales, offs, offs2):
    idx = unstriped(offs)
    idx2 = unstriped(offs2)
    wau = unpack_weight(wa_words, wa_scales, "e2m1")
    wbu = unpack_weight(wb_words, wb_scales, "e4m3")
    xtq = mxq(f64(xt), 0, "e4m3")
    za = wau.T @ xtq
    zb = wbu.T @ xtq
    y = za[:, idx] * zb[:, idx2] - za[:, idx2] * zb[:, idx]
    words, scales = planes(y)
    return y, words, scales

@@ -1,0 +1,159 @@
+from contextlib import ExitStack
+
+import concourse.mybir as mybir
+
+K, T, J, N = 512, 512, 512, 512
+FLOPS = 2 * 2 * K * N * T
+
+F32 = mybir.dt.float32
+BF16 = mybir.dt.bfloat16
+I32 = mybir.dt.int32
+U32 = mybir.dt.uint32
+U16 = mybir.dt.uint16
+U8 = mybir.dt.uint8
+FP8X4 = mybir.dt.float8_e4m3fn_x4
+FP4X4 = mybir.dt.float4_e2m1fn_x4
+MULT = mybir.AluOpType.mult
+SUB = mybir.AluOpType.subtract
+
+P = 128
+PACK = 4
+HALF = T // 2
+X_VEC = 160
+COPY_WINDOW = 704
+MULT_WINDOW = 544
+LAST = 128
+MAIN = J - LAST
+
+
+def tile_list_antisymmetric_pair_pl_kernel(tc, xt, wa_words, wa_scales, wb_words, wb_scales, offs, offs2, out_0, out_1, out_2):
+    nc = tc.nc
+    with ExitStack() as ctx:
+        keep = ctx.enter_context(tc.tile_pool(name="keep", bufs=1))
+        psum = ctx.enter_context(tc.psum_pool(name="psum", bufs=1))
+
+        first = keep.tile([P, J // 16], U16, name="first")
+        second = keep.tile([P, J // 16], U16, name="second")
+        x_raw = [keep.tile([P, PACK, HALF], F32, name=f"x_raw{h}") for h in range(2)]
+        x_grouped = [keep.tile([P, HALF, PACK], BF16, name=f"x_grouped{h}", align_bytes=64) for h in range(2)]
+        x_codes = keep.tile([P, T], U32, name="x_codes", align_bytes=64)
+        x_plane = keep.tile([P, T], U8, name="x_plane", align_bytes=64)
+        wa_raw = keep.tile([P, 2 * N], U8, name="wa_raw")
+        wb_both = keep.tile([P, 5 * N], U8, name="wb_both", tag="wb_then_first_pick")
+        wb_raw = wb_both[:, : 4 * N].bitcast(I32)
+        sb_raw = wb_both[:, 4 * N :]
+        sa_raw = keep.tile([P, N], U8, name="sa_raw")
+        wa_dealt = keep.tile([P, 2 * N], U8, name="wa_dealt", align_bytes=64)
+        wb_dealt = keep.tile([P, N], I32, name="wb_dealt", align_bytes=64)
+        sa_dealt = keep.tile([P, N], U8, name="sa_dealt", align_bytes=64)
+        sb_dealt = keep.tile([P, N], U8, name="sb_dealt", align_bytes=64)
+        za = [keep.tile([P, COPY_WINDOW], F32, name=f"za{t}") for t in range(PACK)]
+        zb = [keep.tile([P, MULT_WINDOW], F32, name=f"zb{t}") for t in range(PACK)]
+        y = keep.tile([P, PACK, J], F32, name="y")
+        y_main = keep.tile([P, MAIN, PACK], BF16, name="y_main", align_bytes=64)
+        y_last = keep.tile([P, LAST, PACK], BF16, name="y_last", align_bytes=64)
+        y_codes = keep.tile([P, J], U32, name="y_codes", align_bytes=64)
+        y_plane = keep.tile([P, J], U8, name="y_plane", align_bytes=64)
+
+        nc.vector.memset(sa_raw[:].bitcast(I32), 0)
+        nc.vector.memset(sb_raw.bitcast(I32), 0)
+        x_rows = xt.rearrange("(p r) c -> p r c", r=PACK)
+
+        def load_scales(tile, rows, at):
+            for q in range(4):
+                nc.sync.dma_start(out=tile[32 * q : 32 * q + 4, at : at + N].bitcast(I32), in_=rows[0, 4 * q : 4 * q + 4, :].bitcast(I32))
+
+        nc.sync.dma_start(first[:], offs)
+        nc.sync.dma_start(out=x_raw[0][:], in_=x_rows[:, :, :HALF])
+        load_scales(sa_raw, wa_scales, 0)
+        nc.sync.dma_start(out=x_raw[1][:], in_=x_rows[:, :, HALF:])
+        nc.sync.dma_start(out=wa_raw[:].bitcast(I32), in_=wa_words[0].bitcast(I32))
+        nc.sync.dma_start(out=wb_raw, in_=wb_words[0].rearrange("p n r -> p (n r)").bitcast(I32))
+        load_scales(wb_both, wb_scales, 4 * N)
+        nc.sync.dma_start(second[:], offs2)
+        for t in range(PACK):
+            nc.vector.memset(za[t][:, T:], 0.0)
+            nc.vector.memset(zb[t][:, T:], 0.0)
+
+        def deal(dst, src, t0, t1):
+            nc.vector.tensor_copy(
+                out=dst.rearrange("p (t m) -> p t m", t=PACK)[:, t0:t1, :],
+                in_=src.rearrange("p (m t) -> p t m", t=PACK)[:, t0:t1, :],
+            )
+
+        def group_x(h):
+            src = x_raw[h][:].rearrange("p r c -> p c r")
+            nc.vector.tensor_copy(out=x_grouped[h][:, :X_VEC, :], in_=src[:, :X_VEC, :])
+            nc.scalar.copy(out=x_grouped[h][:, X_VEC:, :], in_=src[:, X_VEC:, :])
+
+        def quantize(codes, plane, grouped):
+            nc.vector.quantize_mx(out=codes.bitcast(FP8X4), scales=plane, in_=grouped.rearrange("p c r -> p (c r)"))
+
+        def quantize_x(h):
+            cols = slice(h * HALF, (h + 1) * HALF)
+            quantize(x_codes[:, cols], x_plane[:, cols], x_grouped[h][:])
+
+        def product(name, lhsT, lhsT_scale, window, cols):
+            acc = psum.tile([P, cols.stop - cols.start], F32, name=name)
+            nc.tensor.matmul_mx(
+                out=acc[:], lhsT=lhsT, lhsT_scale=lhsT_scale,
+                rhs=x_codes[:, cols].bitcast(FP8X4), rhs_scale=x_plane[:, cols],
+                start=True, stop=True,
+            )
+            nc.scalar.copy(out=window[:, cols], in_=acc[:])
+
+        def make_za(t, name, cols):
+            product(name, wa_dealt[:, 2 * P * t : 2 * P * (t + 1)].bitcast(FP4X4), sa_dealt[:, P * t : P * (t + 1)], za[t], cols)
+
+        def make_zb(t, name):
+            product(name, wb_dealt[:, P * t : P * (t + 1)].bitcast(FP8X4), sb_dealt[:, P * t : P * (t + 1)], zb[t], slice(0, T))
+
+        deal(sa_dealt[:], sa_raw[:], 0, PACK)
+        group_x(0)
+        quantize_x(0)
+        group_x(1)
+        deal(wa_dealt[:].bitcast(U16), wa_raw[:].bitcast(U16), 0, 1)
+        quantize_x(1)
+        make_za(0, "bank0", slice(0, HALF))
+        make_za(0, "bank1", slice(HALF, T))
+        deal(sb_dealt[:], sb_raw, 0, PACK)
+        deal(wb_dealt[:], wb_raw, 0, 1)
+        make_zb(0, "bank2")
+        deal(wa_dealt[:].bitcast(U16), wa_raw[:].bitcast(U16), 1, PACK)
+        deal(wb_dealt[:], wb_raw, 1, PACK)
+        for t in range(1, PACK):
+            make_za(t, f"bank{2 * t + 1}", slice(0, T))
+            make_zb(t, f"bank{(2 * t + 2) % 8}")
+
+        out_rows = out_0.rearrange("(p r) j -> p r j", r=PACK)
+        out_words = out_1[0].rearrange("p j r -> p (j r)").bitcast(I32)
+
+        def look_up(t, cols, u):
+            width = cols.stop - cols.start
+            lo, hi = cols.start // 16, cols.stop // 16
+            a1 = keep.tile([P, width], F32, name=f"a1_{u}", tag="wb_then_first_pick" if u == 0 else f"a1_{u}")
+            a2 = keep.tile([P, width], F32, name=f"a2_{u}")
+            p1 = keep.tile([P, width], F32, name=f"p1_{u}")
+            p2 = keep.tile([P, width], F32, name=f"p2_{u}")
+            nc.vector.tensor_copy(a1[:], za[t][:].indirect(first[:, lo:hi]))
+            nc.vector.tensor_copy(a2[:], za[t][:].indirect(second[:, lo:hi]))
+            nc.vector.tensor_tensor(p1[:], zb[t][:].indirect(second[:, lo:hi]), a1[:], MULT)
+            nc.vector.tensor_tensor(p2[:], zb[t][:].indirect(first[:, lo:hi]), a2[:], MULT)
+            nc.vector.tensor_tensor(y[:, t, cols], p1[:], p2[:], SUB)
+            nc.sync.dma_start(out=out_rows[:, t, cols], in_=y[:, t, cols])
+
+        for t in range(PACK - 1):
+            look_up(t, slice(0, J), t)
+            nc.scalar.copy(out=y_main[:, :, t], in_=y[:, t, :MAIN])
+        look_up(PACK - 1, slice(0, MAIN), PACK - 1)
+        nc.scalar.copy(out=y_main[:, :, PACK - 1], in_=y[:, PACK - 1, :MAIN])
+        look_up(PACK - 1, slice(MAIN, J), PACK)
+        quantize(y_codes[:, :256], y_plane[:, :256], y_main[:, :256, :])
+        quantize(y_codes[:, 256:MAIN], y_plane[:, 256:MAIN], y_main[:, 256:, :])
+        nc.sync.dma_start(out=out_words[:, :MAIN], in_=y_codes[:, :MAIN].bitcast(I32))
+        nc.vector.tensor_copy(out=y_last[:], in_=y[:, :, MAIN:].rearrange("p r c -> p c r"))
+        quantize(y_codes[:, MAIN:], y_plane[:, MAIN:], y_last[:])
+        nc.sync.dma_start(out=out_words[:, MAIN:], in_=y_codes[:, MAIN:].bitcast(I32))
+        for q in range(4):
+            queue = nc.scalar if q % 2 == 0 else nc.sync
+            queue.dma_start(out=out_2[0, 4 * q : 4 * q + 4, :].bitcast(I32), in_=y_plane[32 * q : 32 * q + 4, :].bitcast(I32))

@@ -30,6 +30,7 @@ def tile_list_antisymmetric_pair_pl_kernel(tc, xt, wa_words, wa_scales, wb_words
     nc = tc.nc
     with ExitStack() as ctx:
         keep = ctx.enter_context(tc.tile_pool(name="keep", bufs=1))
+        picks = ctx.enter_context(tc.tile_pool(name="picks", bufs=1))
         psum = ctx.enter_context(tc.psum_pool(name="psum", bufs=1))
 
         first = keep.tile([P, J // 16], U16, name="first")
@@ -39,9 +40,8 @@ def tile_list_antisymmetric_pair_pl_kernel(tc, xt, wa_words, wa_scales, wb_words
         x_codes = keep.tile([P, T], U32, name="x_codes", align_bytes=64)
         x_plane = keep.tile([P, T], U8, name="x_plane", align_bytes=64)
         wa_raw = keep.tile([P, 2 * N], U8, name="wa_raw")
-        wb_both = keep.tile([P, 5 * N], U8, name="wb_both", tag="wb_then_first_pick")
-        wb_raw = wb_both[:, : 4 * N].bitcast(I32)
-        sb_raw = wb_both[:, 4 * N :]
+        wb_raw = keep.tile([P, N], I32, name="wb_raw")
+        sb_raw = picks.tile([P, N], U8, name="sb_raw", offset=4 * J - N // 2)
         sa_raw = keep.tile([P, N], U8, name="sa_raw")
         wa_dealt = keep.tile([P, 2 * N], U8, name="wa_dealt", align_bytes=64)
         wb_dealt = keep.tile([P, N], I32, name="wb_dealt", align_bytes=64)
@@ -56,35 +56,37 @@ def tile_list_antisymmetric_pair_pl_kernel(tc, xt, wa_words, wa_scales, wb_words
         y_plane = keep.tile([P, J], U8, name="y_plane", align_bytes=64)
 
         nc.vector.memset(sa_raw[:].bitcast(I32), 0)
-        nc.vector.memset(sb_raw.bitcast(I32), 0)
+        nc.vector.memset(sb_raw[:].bitcast(I32), 0)
         x_rows = xt.rearrange("(p r) c -> p r c", r=PACK)
 
-        def load_scales(tile, rows, at):
+        def load_scales(plane, rows):
             for q in range(4):
-                nc.sync.dma_start(out=tile[32 * q : 32 * q + 4, at : at + N].bitcast(I32), in_=rows[0, 4 * q : 4 * q + 4, :].bitcast(I32))
+                nc.sync.dma_start(out=plane[32 * q : 32 * q + 4, :].bitcast(I32), in_=rows[0, 4 * q : 4 * q + 4, :].bitcast(I32))
 
         nc.sync.dma_start(first[:], offs)
         nc.sync.dma_start(out=x_raw[0][:], in_=x_rows[:, :, :HALF])
-        load_scales(sa_raw, wa_scales, 0)
+        load_scales(sa_raw, wa_scales)
         nc.sync.dma_start(out=x_raw[1][:], in_=x_rows[:, :, HALF:])
         nc.sync.dma_start(out=wa_raw[:].bitcast(I32), in_=wa_words[0].bitcast(I32))
-        nc.sync.dma_start(out=wb_raw, in_=wb_words[0].rearrange("p n r -> p (n r)").bitcast(I32))
-        load_scales(wb_both, wb_scales, 4 * N)
+        nc.sync.dma_start(out=wb_raw[:], in_=wb_words[0].rearrange("p n r -> p (n r)").bitcast(I32))
+        load_scales(sb_raw, wb_scales)
         nc.sync.dma_start(second[:], offs2)
         for t in range(PACK):
             nc.vector.memset(za[t][:, T:], 0.0)
             nc.vector.memset(zb[t][:, T:], 0.0)
 
-        def deal(dst, src, t0, t1):
+        def deal(dst, src):
             nc.vector.tensor_copy(
-                out=dst.rearrange("p (t m) -> p t m", t=PACK)[:, t0:t1, :],
-                in_=src.rearrange("p (m t) -> p t m", t=PACK)[:, t0:t1, :],
+                out=dst.rearrange("p (t m) -> p m t", t=PACK),
+                in_=src.rearrange("p (m t) -> p m t", t=PACK),
             )
 
+        def group_views(grouped, rows):
+            return grouped.rearrange("p (c i) r -> p c r i", i=4), rows.rearrange("p r (c i) -> p c r i", i=4)
+
         def group_x(h):
-            src = x_raw[h][:].rearrange("p r c -> p c r")
-            nc.vector.tensor_copy(out=x_grouped[h][:, :X_VEC, :], in_=src[:, :X_VEC, :])
-            nc.scalar.copy(out=x_grouped[h][:, X_VEC:, :], in_=src[:, X_VEC:, :])
+            nc.vector.tensor_copy(*group_views(x_grouped[h][:, :X_VEC, :], x_raw[h][:, :, :X_VEC]))
+            nc.scalar.copy(*group_views(x_grouped[h][:, X_VEC:, :], x_raw[h][:, :, X_VEC:]))
 
         def quantize(codes, plane, grouped):
             nc.vector.quantize_mx(out=codes.bitcast(FP8X4), scales=plane, in_=grouped.rearrange("p c r -> p (c r)"))
@@ -108,19 +110,17 @@ def tile_list_antisymmetric_pair_pl_kernel(tc, xt, wa_words, wa_scales, wb_words
         def make_zb(t, name):
             product(name, wb_dealt[:, P * t : P * (t + 1)].bitcast(FP8X4), sb_dealt[:, P * t : P * (t + 1)], zb[t], slice(0, T))
 
-        deal(sa_dealt[:], sa_raw[:], 0, PACK)
+        deal(sa_dealt[:], sa_raw[:])
         group_x(0)
         quantize_x(0)
         group_x(1)
-        deal(wa_dealt[:].bitcast(U16), wa_raw[:].bitcast(U16), 0, 1)
+        deal(wa_dealt[:].bitcast(U16), wa_raw[:].bitcast(U16))
         quantize_x(1)
         make_za(0, "bank0", slice(0, HALF))
         make_za(0, "bank1", slice(HALF, T))
-        deal(sb_dealt[:], sb_raw, 0, PACK)
-        deal(wb_dealt[:], wb_raw, 0, 1)
+        deal(wb_dealt[:], wb_raw[:])
+        deal(sb_dealt[:], sb_raw[:])
         make_zb(0, "bank2")
-        deal(wa_dealt[:].bitcast(U16), wa_raw[:].bitcast(U16), 1, PACK)
-        deal(wb_dealt[:], wb_raw, 1, PACK)
         for t in range(1, PACK):
             make_za(t, f"bank{2 * t + 1}", slice(0, T))
             make_zb(t, f"bank{(2 * t + 2) % 8}")
@@ -131,15 +131,16 @@ def tile_list_antisymmetric_pair_pl_kernel(tc, xt, wa_words, wa_scales, wb_words
         def look_up(t, cols, u):
             width = cols.stop - cols.start
             lo, hi = cols.start // 16, cols.stop // 16
-            a1 = keep.tile([P, width], F32, name=f"a1_{u}", tag="wb_then_first_pick" if u == 0 else f"a1_{u}")
-            a2 = keep.tile([P, width], F32, name=f"a2_{u}")
+            a1 = picks.tile([P, width], F32, name=f"a1_{u}", offset=0)
+            a2 = picks.tile([P, width], F32, name=f"a2_{u}", offset=4 * J)
             p1 = keep.tile([P, width], F32, name=f"p1_{u}")
             p2 = keep.tile([P, width], F32, name=f"p2_{u}")
             nc.vector.tensor_copy(a1[:], za[t][:].indirect(first[:, lo:hi]))
             nc.vector.tensor_copy(a2[:], za[t][:].indirect(second[:, lo:hi]))
             nc.vector.tensor_tensor(p1[:], zb[t][:].indirect(second[:, lo:hi]), a1[:], MULT)
             nc.vector.tensor_tensor(p2[:], zb[t][:].indirect(first[:, lo:hi]), a2[:], MULT)
-            nc.vector.tensor_tensor(y[:, t, cols], p1[:], p2[:], SUB)
+            engine = nc.gpsimd if t < PACK - 1 else nc.vector
+            engine.tensor_tensor(y[:, t, cols], p1[:], p2[:], SUB)
             nc.sync.dma_start(out=out_rows[:, t, cols], in_=y[:, t, cols])
 
         for t in range(PACK - 1):
@@ -151,7 +152,7 @@ def tile_list_antisymmetric_pair_pl_kernel(tc, xt, wa_words, wa_scales, wb_words
         quantize(y_codes[:, :256], y_plane[:, :256], y_main[:, :256, :])
         quantize(y_codes[:, 256:MAIN], y_plane[:, 256:MAIN], y_main[:, 256:, :])
         nc.sync.dma_start(out=out_words[:, :MAIN], in_=y_codes[:, :MAIN].bitcast(I32))
-        nc.vector.tensor_copy(out=y_last[:], in_=y[:, :, MAIN:].rearrange("p r c -> p c r"))
+        nc.vector.tensor_copy(*group_views(y_last[:], y[:, :, MAIN:]))
         quantize(y_codes[:, MAIN:], y_plane[:, MAIN:], y_last[:])
         nc.sync.dma_start(out=out_words[:, MAIN:], in_=y_codes[:, MAIN:].bitcast(I32))
         for q in range(4):

@@ -18,8 +18,8 @@ SUB = mybir.AluOpType.subtract
 
 P = 128
 PACK = 4
-HALF = T // 2
-X_VEC = 160
+X_CHUNKS = (slice(0, 256), slice(256, 512))
+X_VECTOR = (128, 160)
 COPY_WINDOW = 704
 MULT_WINDOW = 544
 LAST = 128
@@ -33,16 +33,17 @@ def tile_list_antisymmetric_pair_pl_kernel(tc, xt, wa_words, wa_scales, wb_words
         picks = ctx.enter_context(tc.tile_pool(name="picks", bufs=1))
         psum = ctx.enter_context(tc.psum_pool(name="psum", bufs=1))
 
+        chunks = range(len(X_CHUNKS))
         first = keep.tile([P, J // 16], U16, name="first")
         second = keep.tile([P, J // 16], U16, name="second")
-        x_raw = [keep.tile([P, PACK, HALF], F32, name=f"x_raw{h}") for h in range(2)]
-        x_grouped = [keep.tile([P, HALF, PACK], BF16, name=f"x_grouped{h}", align_bytes=64) for h in range(2)]
+        x_raw = [keep.tile([P, PACK, c.stop - c.start], F32, name=f"x_raw{c.start}") for c in X_CHUNKS]
+        x_grouped = [keep.tile([P, c.stop - c.start, PACK], BF16, name=f"x_grouped{c.start}", align_bytes=64) for c in X_CHUNKS]
         x_codes = keep.tile([P, T], U32, name="x_codes", align_bytes=64)
         x_plane = keep.tile([P, T], U8, name="x_plane", align_bytes=64)
         wa_raw = keep.tile([P, 2 * N], U8, name="wa_raw")
         wb_raw = keep.tile([P, N], I32, name="wb_raw")
-        sb_raw = picks.tile([P, N], U8, name="sb_raw", offset=4 * J - N // 2)
         sa_raw = keep.tile([P, N], U8, name="sa_raw")
+        sb_raw = picks.tile([P, N], U8, name="sb_raw", offset=4 * J - N // 2)
         wa_dealt = keep.tile([P, 2 * N], U8, name="wa_dealt", align_bytes=64)
         wb_dealt = keep.tile([P, N], I32, name="wb_dealt", align_bytes=64)
         sa_dealt = keep.tile([P, N], U8, name="sa_dealt", align_bytes=64)
@@ -50,8 +51,7 @@ def tile_list_antisymmetric_pair_pl_kernel(tc, xt, wa_words, wa_scales, wb_words
         za = [keep.tile([P, COPY_WINDOW], F32, name=f"za{t}") for t in range(PACK)]
         zb = [keep.tile([P, MULT_WINDOW], F32, name=f"zb{t}") for t in range(PACK)]
         y = keep.tile([P, PACK, J], F32, name="y")
-        y_main = keep.tile([P, MAIN, PACK], BF16, name="y_main", align_bytes=64)
-        y_last = keep.tile([P, LAST, PACK], BF16, name="y_last", align_bytes=64)
+        y_grouped = keep.tile([P, J, PACK], BF16, name="y_grouped", align_bytes=64)
         y_codes = keep.tile([P, J], U32, name="y_codes", align_bytes=64)
         y_plane = keep.tile([P, J], U8, name="y_plane", align_bytes=64)
 
@@ -64,9 +64,10 @@ def tile_list_antisymmetric_pair_pl_kernel(tc, xt, wa_words, wa_scales, wb_words
                 nc.sync.dma_start(out=plane[32 * q : 32 * q + 4, :].bitcast(I32), in_=rows[0, 4 * q : 4 * q + 4, :].bitcast(I32))
 
         nc.sync.dma_start(first[:], offs)
-        nc.sync.dma_start(out=x_raw[0][:], in_=x_rows[:, :, :HALF])
+        nc.sync.dma_start(out=x_raw[0][:], in_=x_rows[:, :, X_CHUNKS[0]])
         load_scales(sa_raw, wa_scales)
-        nc.sync.dma_start(out=x_raw[1][:], in_=x_rows[:, :, HALF:])
+        for h in chunks[1:]:
+            nc.sync.dma_start(out=x_raw[h][:], in_=x_rows[:, :, X_CHUNKS[h]])
         nc.sync.dma_start(out=wa_raw[:].bitcast(I32), in_=wa_words[0].bitcast(I32))
         nc.sync.dma_start(out=wb_raw[:], in_=wb_words[0].rearrange("p n r -> p (n r)").bitcast(I32))
         load_scales(sb_raw, wb_scales)
@@ -85,15 +86,15 @@ def tile_list_antisymmetric_pair_pl_kernel(tc, xt, wa_words, wa_scales, wb_words
             return grouped.rearrange("p (c i) r -> p c r i", i=4), rows.rearrange("p r (c i) -> p c r i", i=4)
 
         def group_x(h):
-            nc.vector.tensor_copy(*group_views(x_grouped[h][:, :X_VEC, :], x_raw[h][:, :, :X_VEC]))
-            nc.scalar.copy(*group_views(x_grouped[h][:, X_VEC:, :], x_raw[h][:, :, X_VEC:]))
+            split = X_VECTOR[h]
+            nc.vector.tensor_copy(*group_views(x_grouped[h][:, :split, :], x_raw[h][:, :, :split]))
+            nc.scalar.copy(*group_views(x_grouped[h][:, split:, :], x_raw[h][:, :, split:]))
 
         def quantize(codes, plane, grouped):
             nc.vector.quantize_mx(out=codes.bitcast(FP8X4), scales=plane, in_=grouped.rearrange("p c r -> p (c r)"))
 
         def quantize_x(h):
-            cols = slice(h * HALF, (h + 1) * HALF)
-            quantize(x_codes[:, cols], x_plane[:, cols], x_grouped[h][:])
+            quantize(x_codes[:, X_CHUNKS[h]], x_plane[:, X_CHUNKS[h]], x_grouped[h][:])
 
         def product(name, lhsT, lhsT_scale, window, cols):
             acc = psum.tile([P, cols.stop - cols.start], F32, name=name)
@@ -116,14 +117,15 @@ def tile_list_antisymmetric_pair_pl_kernel(tc, xt, wa_words, wa_scales, wb_words
         group_x(1)
         deal(wa_dealt[:].bitcast(U16), wa_raw[:].bitcast(U16))
         quantize_x(1)
-        make_za(0, "bank0", slice(0, HALF))
-        make_za(0, "bank1", slice(HALF, T))
+        for h in chunks:
+            make_za(0, f"bank{h}", X_CHUNKS[h])
         deal(wb_dealt[:], wb_raw[:])
         deal(sb_dealt[:], sb_raw[:])
-        make_zb(0, "bank2")
+        free = len(X_CHUNKS)
+        make_zb(0, f"bank{free}")
         for t in range(1, PACK):
-            make_za(t, f"bank{2 * t + 1}", slice(0, T))
-            make_zb(t, f"bank{(2 * t + 2) % 8}")
+            make_za(t, f"bank{(free + 2 * t - 1) % 8}", slice(0, T))
+            make_zb(t, f"bank{(free + 2 * t) % 8}")
 
         out_rows = out_0.rearrange("(p r) j -> p r j", r=PACK)
         out_words = out_1[0].rearrange("p j r -> p (j r)").bitcast(I32)
@@ -142,19 +144,20 @@ def tile_list_antisymmetric_pair_pl_kernel(tc, xt, wa_words, wa_scales, wb_words
             engine = nc.gpsimd if t < PACK - 1 else nc.vector
             engine.tensor_tensor(y[:, t, cols], p1[:], p2[:], SUB)
             nc.sync.dma_start(out=out_rows[:, t, cols], in_=y[:, t, cols])
+            nc.scalar.copy(out=y_grouped[:, cols, t], in_=y[:, t, cols])
+
+        def quantize_y(cols):
+            quantize(y_codes[:, cols], y_plane[:, cols], y_grouped[:, cols, :])
 
         for t in range(PACK - 1):
             look_up(t, slice(0, J), t)
-            nc.scalar.copy(out=y_main[:, :, t], in_=y[:, t, :MAIN])
         look_up(PACK - 1, slice(0, MAIN), PACK - 1)
-        nc.scalar.copy(out=y_main[:, :, PACK - 1], in_=y[:, PACK - 1, :MAIN])
         look_up(PACK - 1, slice(MAIN, J), PACK)
-        quantize(y_codes[:, :256], y_plane[:, :256], y_main[:, :256, :])
-        quantize(y_codes[:, 256:MAIN], y_plane[:, 256:MAIN], y_main[:, 256:, :])
+        quantize_y(slice(0, 256))
+        quantize_y(slice(256, MAIN))
         nc.sync.dma_start(out=out_words[:, :MAIN], in_=y_codes[:, :MAIN].bitcast(I32))
-        nc.vector.tensor_copy(*group_views(y_last[:], y[:, :, MAIN:]))
-        quantize(y_codes[:, MAIN:], y_plane[:, MAIN:], y_last[:])
-        nc.sync.dma_start(out=out_words[:, MAIN:], in_=y_codes[:, MAIN:].bitcast(I32))
+        quantize_y(slice(MAIN, J))
+        nc.scalar.dma_start(out=out_words[:, MAIN:], in_=y_codes[:, MAIN:].bitcast(I32))
         for q in range(4):
-            queue = nc.scalar if q % 2 == 0 else nc.sync
+            queue = nc.sync if q % 2 == 0 else nc.scalar
             queue.dma_start(out=out_2[0, 4 * q : 4 * q + 4, :].bitcast(I32), in_=y_plane[32 * q : 32 * q + 4, :].bitcast(I32))

@@ -18,146 +18,168 @@ SUB = mybir.AluOpType.subtract
 
 P = 128
 PACK = 4
-X_CHUNKS = (slice(0, 256), slice(256, 512))
-X_VECTOR = (128, 160)
-COPY_WINDOW = 704
-MULT_WINDOW = 544
-LAST = 128
-MAIN = J - LAST
+QUADRANTS = 4
+LINE = 4
+PER_COLUMN = 16
+BANKS = 8
+
+TOKEN_HALVES = (slice(0, T // 2), slice(T // 2, T))
+VECTOR_TOKENS = 128
+ZA_COLUMNS = 704
+ZB_COLUMNS = 544
+EARLY_PAIRS = slice(0, 384)
+LATE_PAIRS = slice(384, J)
+EARLY_CALLS = (slice(0, 256), slice(256, 384))
 
 
-def tile_list_antisymmetric_pair_pl_kernel(tc, xt, wa_words, wa_scales, wb_words, wb_scales, offs, offs2, out_0, out_1, out_2):
+def tile_list_antisymmetric_pair_pl_kernel(
+    tc, xt, wa_words, wa_scales, wb_words, wb_scales, offs, offs2, out_0, out_1, out_2
+):
     nc = tc.nc
     with ExitStack() as ctx:
         keep = ctx.enter_context(tc.tile_pool(name="keep", bufs=1))
         picks = ctx.enter_context(tc.tile_pool(name="picks", bufs=1))
         psum = ctx.enter_context(tc.psum_pool(name="psum", bufs=1))
 
-        chunks = range(len(X_CHUNKS))
-        first = keep.tile([P, J // 16], U16, name="first")
-        second = keep.tile([P, J // 16], U16, name="second")
-        x_raw = [keep.tile([P, PACK, c.stop - c.start], F32, name=f"x_raw{c.start}") for c in X_CHUNKS]
-        x_grouped = [keep.tile([P, c.stop - c.start, PACK], BF16, name=f"x_grouped{c.start}", align_bytes=64) for c in X_CHUNKS]
+        idx = keep.tile([P, J // PER_COLUMN], U16, name="idx")
+        idx2 = keep.tile([P, J // PER_COLUMN], U16, name="idx2")
+        x_raw = [keep.tile([P, PACK, T // 2], F32, name=f"x_raw{h}") for h in range(2)]
+        x_grouped = [keep.tile([P, T // 2, PACK], BF16, name=f"x_grouped{h}", align_bytes=64) for h in range(2)]
         x_codes = keep.tile([P, T], U32, name="x_codes", align_bytes=64)
         x_plane = keep.tile([P, T], U8, name="x_plane", align_bytes=64)
         wa_raw = keep.tile([P, 2 * N], U8, name="wa_raw")
         wb_raw = keep.tile([P, N], I32, name="wb_raw")
-        sa_raw = keep.tile([P, N], U8, name="sa_raw")
-        sb_raw = picks.tile([P, N], U8, name="sb_raw", offset=4 * J - N // 2)
+        idx_place, idx2_place = 0, 4 * J
+        wb_plane_raw = picks.tile([P, N], U8, name="wb_plane_raw", offset=idx2_place - N // 2)
+        wa_plane_raw = keep.tile([P, N], U8, name="wa_plane_raw")
         wa_dealt = keep.tile([P, 2 * N], U8, name="wa_dealt", align_bytes=64)
         wb_dealt = keep.tile([P, N], I32, name="wb_dealt", align_bytes=64)
-        sa_dealt = keep.tile([P, N], U8, name="sa_dealt", align_bytes=64)
-        sb_dealt = keep.tile([P, N], U8, name="sb_dealt", align_bytes=64)
-        za = [keep.tile([P, COPY_WINDOW], F32, name=f"za{t}") for t in range(PACK)]
-        zb = [keep.tile([P, MULT_WINDOW], F32, name=f"zb{t}") for t in range(PACK)]
+        wa_plane = keep.tile([P, N], U8, name="wa_plane", align_bytes=64)
+        wb_plane = keep.tile([P, N], U8, name="wb_plane", align_bytes=64)
+        za = [keep.tile([P, ZA_COLUMNS], F32, name=f"za{r}") for r in range(PACK)]
+        zb = [keep.tile([P, ZB_COLUMNS], F32, name=f"zb{r}") for r in range(PACK)]
         y = keep.tile([P, PACK, J], F32, name="y")
         y_grouped = keep.tile([P, J, PACK], BF16, name="y_grouped", align_bytes=64)
         y_codes = keep.tile([P, J], U32, name="y_codes", align_bytes=64)
         y_plane = keep.tile([P, J], U8, name="y_plane", align_bytes=64)
 
-        nc.vector.memset(sa_raw[:].bitcast(I32), 0)
-        nc.vector.memset(sb_raw[:].bitcast(I32), 0)
+        def plane_rows(plane, q):
+            return plane[32 * q : 32 * q + 4, :].bitcast(I32)
+
+        def scale_rows(scales, q):
+            return scales[0, 4 * q : 4 * q + 4, :].bitcast(I32)
+
+        def load_plane(plane, scales):
+            for q in range(QUADRANTS):
+                nc.sync.dma_start(out=plane_rows(plane, q), in_=scale_rows(scales, q))
+
+        nc.vector.memset(wa_plane_raw[:].bitcast(I32), 0)
+        nc.vector.memset(wb_plane_raw[:].bitcast(I32), 0)
+
         x_rows = xt.rearrange("(p r) c -> p r c", r=PACK)
-
-        def load_scales(plane, rows):
-            for q in range(4):
-                nc.sync.dma_start(out=plane[32 * q : 32 * q + 4, :].bitcast(I32), in_=rows[0, 4 * q : 4 * q + 4, :].bitcast(I32))
-
-        nc.sync.dma_start(first[:], offs)
-        nc.sync.dma_start(out=x_raw[0][:], in_=x_rows[:, :, X_CHUNKS[0]])
-        load_scales(sa_raw, wa_scales)
-        for h in chunks[1:]:
-            nc.sync.dma_start(out=x_raw[h][:], in_=x_rows[:, :, X_CHUNKS[h]])
+        nc.sync.dma_start(out=x_raw[0][:], in_=x_rows[:, :, TOKEN_HALVES[0]])
+        load_plane(wa_plane_raw, wa_scales)
+        nc.sync.dma_start(idx[:], offs)
+        nc.sync.dma_start(out=x_raw[1][:], in_=x_rows[:, :, TOKEN_HALVES[1]])
         nc.sync.dma_start(out=wa_raw[:].bitcast(I32), in_=wa_words[0].bitcast(I32))
         nc.sync.dma_start(out=wb_raw[:], in_=wb_words[0].rearrange("p n r -> p (n r)").bitcast(I32))
-        load_scales(sb_raw, wb_scales)
-        nc.sync.dma_start(second[:], offs2)
-        for t in range(PACK):
-            nc.vector.memset(za[t][:, T:], 0.0)
-            nc.vector.memset(zb[t][:, T:], 0.0)
+        load_plane(wb_plane_raw, wb_scales)
+        nc.sync.dma_start(idx2[:], offs2)
+
+        for r in range(PACK):
+            nc.vector.memset(za[r][:, T:], 0.0)
+            nc.vector.memset(zb[r][:, T:], 0.0)
 
         def deal(dst, src):
             nc.vector.tensor_copy(
-                out=dst.rearrange("p (t m) -> p m t", t=PACK),
-                in_=src.rearrange("p (m t) -> p m t", t=PACK),
+                out=dst.rearrange("p (r m) -> p m r", r=PACK),
+                in_=src.rearrange("p (m r) -> p m r", r=PACK),
             )
 
         def group_views(grouped, rows):
-            return grouped.rearrange("p (c i) r -> p c r i", i=4), rows.rearrange("p r (c i) -> p c r i", i=4)
+            return (
+                grouped.rearrange("p (c i) r -> p c r i", i=LINE),
+                rows.rearrange("p r (c i) -> p c r i", i=LINE),
+            )
 
         def group_x(h):
-            split = X_VECTOR[h]
-            nc.vector.tensor_copy(*group_views(x_grouped[h][:, :split, :], x_raw[h][:, :, :split]))
-            nc.scalar.copy(*group_views(x_grouped[h][:, split:, :], x_raw[h][:, :, split:]))
+            nc.vector.tensor_copy(*group_views(x_grouped[h][:, :VECTOR_TOKENS, :], x_raw[h][:, :, :VECTOR_TOKENS]))
+            nc.scalar.copy(*group_views(x_grouped[h][:, VECTOR_TOKENS:, :], x_raw[h][:, :, VECTOR_TOKENS:]))
 
         def quantize(codes, plane, grouped):
             nc.vector.quantize_mx(out=codes.bitcast(FP8X4), scales=plane, in_=grouped.rearrange("p c r -> p (c r)"))
 
         def quantize_x(h):
-            quantize(x_codes[:, X_CHUNKS[h]], x_plane[:, X_CHUNKS[h]], x_grouped[h][:])
+            quantize(x_codes[:, TOKEN_HALVES[h]], x_plane[:, TOKEN_HALVES[h]], x_grouped[h][:])
 
-        def product(name, lhsT, lhsT_scale, window, cols):
-            acc = psum.tile([P, cols.stop - cols.start], F32, name=name)
+        def product(number, lhsT, lhsT_scale, z, tokens):
+            acc = psum.tile([P, tokens.stop - tokens.start], F32, name=f"bank{number % BANKS}")
             nc.tensor.matmul_mx(
-                out=acc[:], lhsT=lhsT, lhsT_scale=lhsT_scale,
-                rhs=x_codes[:, cols].bitcast(FP8X4), rhs_scale=x_plane[:, cols],
-                start=True, stop=True,
+                out=acc[:],
+                lhsT=lhsT,
+                lhsT_scale=lhsT_scale,
+                rhs=x_codes[:, tokens].bitcast(FP8X4),
+                rhs_scale=x_plane[:, tokens],
+                start=True,
+                stop=True,
             )
-            nc.scalar.copy(out=window[:, cols], in_=acc[:])
+            nc.scalar.copy(out=z[:, tokens], in_=acc[:])
 
-        def make_za(t, name, cols):
-            product(name, wa_dealt[:, 2 * P * t : 2 * P * (t + 1)].bitcast(FP4X4), sa_dealt[:, P * t : P * (t + 1)], za[t], cols)
+        def make_za(number, r, tokens):
+            words = wa_dealt[:, 2 * P * r : 2 * P * (r + 1)].bitcast(FP4X4)
+            product(number, words, wa_plane[:, P * r : P * (r + 1)], za[r], tokens)
 
-        def make_zb(t, name):
-            product(name, wb_dealt[:, P * t : P * (t + 1)].bitcast(FP8X4), sb_dealt[:, P * t : P * (t + 1)], zb[t], slice(0, T))
+        def make_zb(number, r):
+            words = wb_dealt[:, P * r : P * (r + 1)].bitcast(FP8X4)
+            product(number, words, wb_plane[:, P * r : P * (r + 1)], zb[r], slice(0, T))
 
-        deal(sa_dealt[:], sa_raw[:])
+        deal(wa_plane[:], wa_plane_raw[:])
         group_x(0)
         quantize_x(0)
         group_x(1)
         deal(wa_dealt[:].bitcast(U16), wa_raw[:].bitcast(U16))
         quantize_x(1)
-        for h in chunks:
-            make_za(0, f"bank{h}", X_CHUNKS[h])
+        for h in range(2):
+            make_za(h, 0, TOKEN_HALVES[h])
         deal(wb_dealt[:], wb_raw[:])
-        deal(sb_dealt[:], sb_raw[:])
-        free = len(X_CHUNKS)
-        make_zb(0, f"bank{free}")
-        for t in range(1, PACK):
-            make_za(t, f"bank{(free + 2 * t - 1) % 8}", slice(0, T))
-            make_zb(t, f"bank{(free + 2 * t) % 8}")
+        deal(wb_plane[:], wb_plane_raw[:])
+        make_zb(2, 0)
+        for r in range(1, PACK):
+            make_za(2 * r + 1, r, slice(0, T))
+            make_zb(2 * r + 2, r)
 
         out_rows = out_0.rearrange("(p r) j -> p r j", r=PACK)
         out_words = out_1[0].rearrange("p j r -> p (j r)").bitcast(I32)
 
-        def look_up(t, cols, u):
-            width = cols.stop - cols.start
-            lo, hi = cols.start // 16, cols.stop // 16
-            a1 = picks.tile([P, width], F32, name=f"a1_{u}", offset=0)
-            a2 = picks.tile([P, width], F32, name=f"a2_{u}", offset=4 * J)
-            p1 = keep.tile([P, width], F32, name=f"p1_{u}")
-            p2 = keep.tile([P, width], F32, name=f"p2_{u}")
-            nc.vector.tensor_copy(a1[:], za[t][:].indirect(first[:, lo:hi]))
-            nc.vector.tensor_copy(a2[:], za[t][:].indirect(second[:, lo:hi]))
-            nc.vector.tensor_tensor(p1[:], zb[t][:].indirect(second[:, lo:hi]), a1[:], MULT)
-            nc.vector.tensor_tensor(p2[:], zb[t][:].indirect(first[:, lo:hi]), a2[:], MULT)
-            engine = nc.gpsimd if t < PACK - 1 else nc.vector
-            engine.tensor_tensor(y[:, t, cols], p1[:], p2[:], SUB)
-            nc.sync.dma_start(out=out_rows[:, t, cols], in_=y[:, t, cols])
-            nc.scalar.copy(out=y_grouped[:, cols, t], in_=y[:, t, cols])
+        def look_up(r, pairs, subtracts):
+            width = pairs.stop - pairs.start
+            entries = slice(pairs.start // PER_COLUMN, pairs.stop // PER_COLUMN)
+            label = f"{r}_{pairs.start}"
+            za_idx = picks.tile([P, width], F32, name=f"za_idx{label}", offset=idx_place)
+            za_idx2 = picks.tile([P, width], F32, name=f"za_idx2{label}", offset=idx2_place)
+            plus = keep.tile([P, width], F32, name=f"plus{label}")
+            minus = keep.tile([P, width], F32, name=f"minus{label}")
+            nc.vector.tensor_copy(za_idx[:], za[r][:].indirect(idx[:, entries]))
+            nc.vector.tensor_copy(za_idx2[:], za[r][:].indirect(idx2[:, entries]))
+            nc.vector.tensor_tensor(plus[:], zb[r][:].indirect(idx2[:, entries]), za_idx[:], MULT)
+            nc.vector.tensor_tensor(minus[:], zb[r][:].indirect(idx[:, entries]), za_idx2[:], MULT)
+            subtracts.tensor_tensor(y[:, r, pairs], plus[:], minus[:], SUB)
+            nc.sync.dma_start(out=out_rows[:, r, pairs], in_=y[:, r, pairs])
+            nc.scalar.copy(out=y_grouped[:, pairs, r], in_=y[:, r, pairs])
 
-        def quantize_y(cols):
-            quantize(y_codes[:, cols], y_plane[:, cols], y_grouped[:, cols, :])
+        def quantize_y(pairs):
+            quantize(y_codes[:, pairs], y_plane[:, pairs], y_grouped[:, pairs, :])
 
-        for t in range(PACK - 1):
-            look_up(t, slice(0, J), t)
-        look_up(PACK - 1, slice(0, MAIN), PACK - 1)
-        look_up(PACK - 1, slice(MAIN, J), PACK)
-        quantize_y(slice(0, 256))
-        quantize_y(slice(256, MAIN))
-        nc.sync.dma_start(out=out_words[:, :MAIN], in_=y_codes[:, :MAIN].bitcast(I32))
-        quantize_y(slice(MAIN, J))
-        nc.scalar.dma_start(out=out_words[:, MAIN:], in_=y_codes[:, MAIN:].bitcast(I32))
-        for q in range(4):
+        for r in range(PACK - 1):
+            look_up(r, slice(0, J), nc.gpsimd)
+        look_up(PACK - 1, EARLY_PAIRS, nc.vector)
+        look_up(PACK - 1, LATE_PAIRS, nc.vector)
+
+        for pairs in EARLY_CALLS:
+            quantize_y(pairs)
+        nc.sync.dma_start(out=out_words[:, EARLY_PAIRS], in_=y_codes[:, EARLY_PAIRS].bitcast(I32))
+        quantize_y(LATE_PAIRS)
+        nc.scalar.dma_start(out=out_words[:, LATE_PAIRS], in_=y_codes[:, LATE_PAIRS].bitcast(I32))
+        for q in range(QUADRANTS):
             queue = nc.sync if q % 2 == 0 else nc.scalar
-            queue.dma_start(out=out_2[0, 4 * q : 4 * q + 4, :].bitcast(I32), in_=y_plane[32 * q : 32 * q + 4, :].bitcast(I32))
+            queue.dma_start(out=scale_rows(out_2, q), in_=plane_rows(y_plane, q))

from contextlib import ExitStack

import concourse.mybir as mybir

K, T, J, N = 512, 512, 512, 512
FLOPS = 2 * 2 * K * N * T

F32 = mybir.dt.float32
BF16 = mybir.dt.bfloat16
I32 = mybir.dt.int32
U32 = mybir.dt.uint32
U16 = mybir.dt.uint16
U8 = mybir.dt.uint8
FP8X4 = mybir.dt.float8_e4m3fn_x4
FP4X4 = mybir.dt.float4_e2m1fn_x4
MULT = mybir.AluOpType.mult
SUB = mybir.AluOpType.subtract

P = 128
PACK = 4
QUADRANTS = 4
LINE = 4
PER_COLUMN = 16
BANKS = 8

TOKEN_HALVES = (slice(0, T // 2), slice(T // 2, T))
VECTOR_TOKENS = 128
ZA_COLUMNS = 704
ZB_COLUMNS = 544
EARLY_PAIRS = slice(0, 384)
LATE_PAIRS = slice(384, J)
EARLY_CALLS = (slice(0, 256), slice(256, 384))


def tile_list_antisymmetric_pair_pl_kernel(
    tc, xt, wa_words, wa_scales, wb_words, wb_scales, offs, offs2, out_0, out_1, out_2
):
    nc = tc.nc
    with ExitStack() as ctx:
        keep = ctx.enter_context(tc.tile_pool(name="keep", bufs=1))
        picks = ctx.enter_context(tc.tile_pool(name="picks", bufs=1))
        psum = ctx.enter_context(tc.psum_pool(name="psum", bufs=1))

        idx = keep.tile([P, J // PER_COLUMN], U16, name="idx")
        idx2 = keep.tile([P, J // PER_COLUMN], U16, name="idx2")
        x_raw = [keep.tile([P, PACK, T // 2], F32, name=f"x_raw{h}") for h in range(2)]
        x_grouped = [keep.tile([P, T // 2, PACK], BF16, name=f"x_grouped{h}", align_bytes=64) for h in range(2)]
        x_codes = keep.tile([P, T], U32, name="x_codes", align_bytes=64)
        x_plane = keep.tile([P, T], U8, name="x_plane", align_bytes=64)
        wa_raw = keep.tile([P, 2 * N], U8, name="wa_raw")
        wb_raw = keep.tile([P, N], I32, name="wb_raw")
        idx_place, idx2_place = 0, 4 * J
        wb_plane_raw = picks.tile([P, N], U8, name="wb_plane_raw", offset=idx2_place - N // 2)
        wa_plane_raw = keep.tile([P, N], U8, name="wa_plane_raw")
        wa_dealt = keep.tile([P, 2 * N], U8, name="wa_dealt", align_bytes=64)
        wb_dealt = keep.tile([P, N], I32, name="wb_dealt", align_bytes=64)
        wa_plane = keep.tile([P, N], U8, name="wa_plane", align_bytes=64)
        wb_plane = keep.tile([P, N], U8, name="wb_plane", align_bytes=64)
        za = [keep.tile([P, ZA_COLUMNS], F32, name=f"za{r}") for r in range(PACK)]
        zb = [keep.tile([P, ZB_COLUMNS], F32, name=f"zb{r}") for r in range(PACK)]
        y = keep.tile([P, PACK, J], F32, name="y")
        y_grouped = keep.tile([P, J, PACK], BF16, name="y_grouped", align_bytes=64)
        y_codes = keep.tile([P, J], U32, name="y_codes", align_bytes=64)
        y_plane = keep.tile([P, J], U8, name="y_plane", align_bytes=64)

        def plane_rows(plane, q):
            return plane[32 * q : 32 * q + 4, :].bitcast(I32)

        def scale_rows(scales, q):
            return scales[0, 4 * q : 4 * q + 4, :].bitcast(I32)

        def load_plane(plane, scales):
            for q in range(QUADRANTS):
                nc.sync.dma_start(out=plane_rows(plane, q), in_=scale_rows(scales, q))

        nc.vector.memset(wa_plane_raw[:].bitcast(I32), 0)
        nc.vector.memset(wb_plane_raw[:].bitcast(I32), 0)

        x_rows = xt.rearrange("(p r) c -> p r c", r=PACK)
        nc.sync.dma_start(out=x_raw[0][:], in_=x_rows[:, :, TOKEN_HALVES[0]])
        load_plane(wa_plane_raw, wa_scales)
        nc.sync.dma_start(idx[:], offs)
        nc.sync.dma_start(out=x_raw[1][:], in_=x_rows[:, :, TOKEN_HALVES[1]])
        nc.sync.dma_start(out=wa_raw[:].bitcast(I32), in_=wa_words[0].bitcast(I32))
        nc.sync.dma_start(out=wb_raw[:], in_=wb_words[0].rearrange("p n r -> p (n r)").bitcast(I32))
        load_plane(wb_plane_raw, wb_scales)
        nc.sync.dma_start(idx2[:], offs2)

        for r in range(PACK):
            nc.vector.memset(za[r][:, T:], 0.0)
            nc.vector.memset(zb[r][:, T:], 0.0)

        def deal(dst, src):
            nc.vector.tensor_copy(
                out=dst.rearrange("p (r m) -> p m r", r=PACK),
                in_=src.rearrange("p (m r) -> p m r", r=PACK),
            )

        def group_views(grouped, rows):
            return (
                grouped.rearrange("p (c i) r -> p c r i", i=LINE),
                rows.rearrange("p r (c i) -> p c r i", i=LINE),
            )

        def group_x(h):
            nc.vector.tensor_copy(*group_views(x_grouped[h][:, :VECTOR_TOKENS, :], x_raw[h][:, :, :VECTOR_TOKENS]))
            nc.scalar.copy(*group_views(x_grouped[h][:, VECTOR_TOKENS:, :], x_raw[h][:, :, VECTOR_TOKENS:]))

        def quantize(codes, plane, grouped):
            nc.vector.quantize_mx(out=codes.bitcast(FP8X4), scales=plane, in_=grouped.rearrange("p c r -> p (c r)"))

        def quantize_x(h):
            quantize(x_codes[:, TOKEN_HALVES[h]], x_plane[:, TOKEN_HALVES[h]], x_grouped[h][:])

        def product(number, lhsT, lhsT_scale, z, tokens):
            acc = psum.tile([P, tokens.stop - tokens.start], F32, name=f"bank{number % BANKS}")
            nc.tensor.matmul_mx(
                out=acc[:],
                lhsT=lhsT,
                lhsT_scale=lhsT_scale,
                rhs=x_codes[:, tokens].bitcast(FP8X4),
                rhs_scale=x_plane[:, tokens],
                start=True,
                stop=True,
            )
            nc.scalar.copy(out=z[:, tokens], in_=acc[:])

        def make_za(number, r, tokens):
            words = wa_dealt[:, 2 * P * r : 2 * P * (r + 1)].bitcast(FP4X4)
            product(number, words, wa_plane[:, P * r : P * (r + 1)], za[r], tokens)

        def make_zb(number, r):
            words = wb_dealt[:, P * r : P * (r + 1)].bitcast(FP8X4)
            product(number, words, wb_plane[:, P * r : P * (r + 1)], zb[r], slice(0, T))

        deal(wa_plane[:], wa_plane_raw[:])
        group_x(0)
        quantize_x(0)
        group_x(1)
        deal(wa_dealt[:].bitcast(U16), wa_raw[:].bitcast(U16))
        quantize_x(1)
        for h in range(2):
            make_za(h, 0, TOKEN_HALVES[h])
        deal(wb_dealt[:], wb_raw[:])
        deal(wb_plane[:], wb_plane_raw[:])
        make_zb(2, 0)
        for r in range(1, PACK):
            make_za(2 * r + 1, r, slice(0, T))
            make_zb(2 * r + 2, r)

        out_rows = out_0.rearrange("(p r) j -> p r j", r=PACK)
        out_words = out_1[0].rearrange("p j r -> p (j r)").bitcast(I32)

        def look_up(r, pairs, subtracts):
            width = pairs.stop - pairs.start
            entries = slice(pairs.start // PER_COLUMN, pairs.stop // PER_COLUMN)
            label = f"{r}_{pairs.start}"
            za_idx = picks.tile([P, width], F32, name=f"za_idx{label}", offset=idx_place)
            za_idx2 = picks.tile([P, width], F32, name=f"za_idx2{label}", offset=idx2_place)
            plus = keep.tile([P, width], F32, name=f"plus{label}")
            minus = keep.tile([P, width], F32, name=f"minus{label}")
            nc.vector.tensor_copy(za_idx[:], za[r][:].indirect(idx[:, entries]))
            nc.vector.tensor_copy(za_idx2[:], za[r][:].indirect(idx2[:, entries]))
            nc.vector.tensor_tensor(plus[:], zb[r][:].indirect(idx2[:, entries]), za_idx[:], MULT)
            nc.vector.tensor_tensor(minus[:], zb[r][:].indirect(idx[:, entries]), za_idx2[:], MULT)
            subtracts.tensor_tensor(y[:, r, pairs], plus[:], minus[:], SUB)
            nc.sync.dma_start(out=out_rows[:, r, pairs], in_=y[:, r, pairs])
            nc.scalar.copy(out=y_grouped[:, pairs, r], in_=y[:, r, pairs])

        def quantize_y(pairs):
            quantize(y_codes[:, pairs], y_plane[:, pairs], y_grouped[:, pairs, :])

        for r in range(PACK - 1):
            look_up(r, slice(0, J), nc.gpsimd)
        look_up(PACK - 1, EARLY_PAIRS, nc.vector)
        look_up(PACK - 1, LATE_PAIRS, nc.vector)

        for pairs in EARLY_CALLS:
            quantize_y(pairs)
        nc.sync.dma_start(out=out_words[:, EARLY_PAIRS], in_=y_codes[:, EARLY_PAIRS].bitcast(I32))
        quantize_y(LATE_PAIRS)
        nc.scalar.dma_start(out=out_words[:, LATE_PAIRS], in_=y_codes[:, LATE_PAIRS].bitcast(I32))
        for q in range(QUADRANTS):
            queue = nc.sync if q % 2 == 0 else nc.scalar
            queue.dma_start(out=scale_rows(out_2, q), in_=plane_rows(y_plane, q))
